import numpy as np
import ml_dtypes


def mxq(x, axis, fmt="e4m3"):
    dtype, down = {"e4m3": (ml_dtypes.float8_e4m3fn, 7), "e5m2": (ml_dtypes.float8_e5m2, 14)}[fmt]
    v = np.moveaxis(np.asarray(x, np.float32).astype(ml_dtypes.bfloat16).astype(np.float64), axis, -1)
    blocks = v.reshape(v.shape[:-1] + (-1, 32))
    amax = np.abs(blocks).max(-1, keepdims=True)
    byte = np.maximum(np.where(amax > 0, np.frexp(amax)[1] - 1 + 127, 0) - down, 1)
    scale = np.exp2(byte - 127.0)
    codes = (blocks / scale).astype(np.float32).astype(dtype).astype(np.float64)
    return np.moveaxis((codes * scale).reshape(v.shape), -1, axis)


WIDE = False


def mx_kscale(k):
    if not WIDE:
        return np.ones(k)
    levels = np.array([10, -10, 5, -5, 0])
    if k % 512:
        return np.exp2(np.random.permutation(np.resize(levels, k // 32))).repeat(32)
    a = np.empty((k // 512, 16))
    for p in range(k // 512):
        a[p, :8] = np.random.permutation(np.resize(levels, 8))
        for g in range(8):
            far = levels[np.abs(levels - a[p, g]) >= 10]
            a[p, g + 8] = far[np.random.randint(len(far))]
    return np.exp2(a.ravel()).repeat(32)


BF16 = ml_dtypes.bfloat16


def bf(x):
    return np.asarray(x, np.float32).astype(BF16)


def f64(x):
    return np.asarray(x).astype(np.float64)

def planes(Y):
    n, m = Y.shape
    b = f64(bf(Y)).reshape(n // 32, 32, m)
    amax = np.abs(b).max(1)
    byte = np.clip(np.where(amax > 0, np.frexp(amax)[1] - 1 + 127 - 7, 1), 1, 254)
    codes = (b * np.exp2(127.0 - byte)[:, None, :]).reshape(n, m).astype(np.float32).astype(ml_dtypes.float8_e4m3fn).view(np.uint8)
    words = codes.reshape(n // 512, 128, 4, m).transpose(0, 1, 3, 2)
    return np.ascontiguousarray(words), np.ascontiguousarray(byte.astype(np.uint8).reshape(n // 512, 16, m))


M, S, N = 1024, 1024, 2048

SIZE_SPREAD = 0.8
STATE_STD = 0.7


def setup_inputs():
    s = mx_kscale(S)
    spread = np.exp(SIZE_SPREAD * np.random.randn(N))
    x = STATE_STD * np.random.randn(M, S)
    x_ref = STATE_STD * np.random.randn(M, S)
    gain = np.random.randn(S, N) / np.sqrt(S) * spread
    u_ref = 0.4 * np.random.randn(M, N) * spread
    u_lo = -1.0 * np.exp(0.1 * np.random.randn(N)) * spread
    u_hi = 1.2 * np.exp(0.1 * np.random.randn(N)) * spread
    return {
        "x": bf(x * s),
        "x_ref": bf(x_ref * s),
        "gain": bf(gain / s[:, None]),
        "u_ref": bf(u_ref),
        "u_lo": bf(u_lo),
        "u_hi": bf(u_hi),
    }


def reference(x, x_ref, gain, u_ref, u_lo, u_hi):
    err = f64(x_ref) - f64(x)
    fb = mxq(err, 1, "e4m3") @ mxq(f64(gain), 0, "e4m3")
    y = np.minimum(np.maximum(fb + f64(u_ref), f64(u_lo)), f64(u_hi))
    Y = y.T
    words, scales = planes(Y)
    return y, words, scales

@@ -1,0 +1,242 @@
+from contextlib import ExitStack
+
+import concourse.mybir as mybir
+from concourse.masks import make_identity
+
+M, S, N = 1024, 1024, 2048
+FLOPS = 2 * M * S * N
+
+F32 = mybir.dt.float32
+BF16 = mybir.dt.bfloat16
+I32 = mybir.dt.int32
+U32 = mybir.dt.uint32
+U8 = mybir.dt.uint8
+FP8X4 = mybir.dt.float8_e4m3fn_x4
+ALU = mybir.AluOpType
+
+P = 128
+PACK = 4
+GROUP = P * PACK
+KP = S // GROUP
+G = N // GROUP
+ROWS = 256
+B = ROWS // P
+C = M // ROWS
+FB_BANKS, BACK_BANKS, TURN_BANKS = 3, 3, 2
+ORDER = """
+lg:001 lg:101 lx:0 lu:002 lg:111 lg:011 lx:1 lu:102 lg:022 lg:122 lu:022 lu:122 lx:2 lu:204 lx:3 lu:304 gi:S00
+gi:V10 gq:00 gq:10 sub:00 sub:01 et:00 et:01 ec:S00 ec:S01 gi:V11 ut:00 ut:01 uc:S00 eq:00 eq:01 gi:S01 gq:11
+mm:000 uc:V01 mm:001 add:000 sub:11 sub:10 et:11 gq:01 et:10 add:001 ec:S11 mm:010 cl:V000 ec:S10 cl:V001
+mm:011 eq:11 eq:10 yi:S00 ut:10 add:010 yt:000 gi:V02 yt:001 uc:S10 ut:11 yc:S000 mm:100 add:011 uc:S11 mm:101
+yq:00 yc:S001 cl:V010 mm:110 cl:V011 gi:S12 add:100 ut:02 yi:V01 yt:010 yt:011 add:101 ut:03 gq:02 mm:111
+yc:S010 gq:12 yc:S011 sy:010 yq:01 uc:S02 cl:V100 mm:020 sy:011 sc:01 cl:V101 gi:S13 add:110 ut:12 yi:V10
+yt:100 yt:101 add:111 mm:021 gi:V03 yc:S100 mm:120 uc:S03 gq:13 yc:S101 ut:13 gq:03 uc:S12 yq:10 cl:V110
+uc:S13 ut:20 cl:V111 add:020 ut:21 yi:S11 sub:21 yt:110 yt:111 add:021 mm:030 yc:S110 yq:11 yc:S111 mm:031
+cl:V020 sy:110 sc:11 cl:V021 uc:S20 sub:20 sy:111 yt:020 yi:S02 add:030 yt:021 et:21 add:120 yc:S020 add:031
+mm:121 ec:S21 yq:02 cl:V030 mm:130 yc:S021 cl:V031 eq:21 mm:131 uc:S21 yi:V03 yt:030 et:20 add:121 yc:S030
+yt:031 yq:03 cl:V120 ut:22 ec:S20 sc:03 sy:030 cl:V121 yc:S031 add:130 yt:120 eq:20 yi:S12 yt:121 sy:031
+add:131 ut:23 cl:V130 mm:200 yc:S120 cl:V131 yq:12 mm:201 uc:S22 yi:V13 mm:210 yc:S121 add:200 yt:130 uc:S23
+yq:13 yt:131 add:201 yc:S130 mm:211 sc:13 cl:V200 yc:S131 ut:30 cl:V201 sy:130 sub:31 mm:220 yi:S20 sy:131
+sub:30 yt:200 add:210 yt:201 uc:S30 et:30 yq:20 yc:S200 add:211 mm:221 ec:S30 cl:V210 et:31 cl:V211 yc:S201
+add:220 yt:210 yi:S21 eq:30 yt:211 add:221 ut:31 cl:V220 mm:230 ec:S31 cl:V221 yq:21 yc:S210 mm:231 eq:31
+yc:S211 sc:21 yt:220 yi:V22 sy:210 yt:221 uc:S31 add:230 ut:32 sy:211 yc:S220 yq:22 mm:300 add:231 uc:S32
+mm:301 cl:V230 yc:S221 cl:V231 mm:310 add:300 yi:S23 yt:230 add:310 yt:231 ut:33 add:301 yc:S230 mm:311 yq:23
+yc:S231 cl:V300 sy:230 mm:320 sc:23 cl:V301 ss:0 uc:S33 add:311 mm:321 sy:231 yi:S30 cl:V310 yt:300 cl:V311
+yt:301 add:320 mm:330 yc:S300 yi:V31 mm:331 yc:S301 yq:30 yt:310 add:321 yt:311 yq:31 yc:S310 cl:V320 sc:31
+cl:V321 yc:S311 sy:310 add:330 yi:S32 yt:320 sy:311 yt:321 add:331 cl:V330 yc:S320 cl:V331 yq:32 yc:S321
+sy:320 yt:330 yi:V33 yt:331 yc:S330 sy:321 yq:33 yc:S331 sc:33 sy:330 ss:1 sy:331
+"""
+
+
+def tile_saturated_state_feedback_g1_kernel(tc, x, x_ref, gain, u_ref, u_lo, u_hi, out_0, out_1, out_2):
+    nc = tc.nc
+    with ExitStack() as ctx:
+        keep = ctx.enter_context(tc.tile_pool(name="keep", bufs=1))
+        work = ctx.enter_context(tc.tile_pool(name="work", bufs=3))
+        psum = ctx.enter_context(tc.psum_pool(name="psum", bufs=2))
+        ctx.enter_context(tc.manual_schedule())
+
+        ident = keep.tile([P, P], F32, name="ident")
+        lim_raw = keep.tile([P, 2, G, PACK], BF16, name="lim_raw")
+        lim = keep.tile([P, 2, G, PACK], F32, name="lim")
+        gain_codes = keep.tile([P, KP, N], U32, name="gain_codes", align_bytes=64)
+        gain_scales = keep.tile([P, KP, N], U8, name="gain_scales", align_bytes=64)
+        err_codes = keep.tile([P, KP, M], U32, name="err_codes", align_bytes=64)
+        err_scales = keep.tile([P, KP, M], U8, name="err_scales", align_bytes=64)
+        early_scales = keep.tile([P, G, M - ROWS], U8, name="early_scales", align_bytes=64)
+        last_scales = keep.tile([P, G, ROWS], U8, name="last_scales", align_bytes=64)
+
+        gain_raw, x_raw, xr_raw, u_raw = {}, {}, {}, {}
+        gain_il, err, err_t, err_ps, u_ps, u_t, fb, y_t, y_il, y_ps, y_rows, y_codes = ({} for k in range(12))
+
+        def copy(eng, dst, src):
+            if eng == "V":
+                nc.vector.tensor_copy(out=dst, in_=src)
+            else:
+                nc.scalar.copy(out=dst, in_=src)
+
+        def load_gain(kp, g0, ng):
+            t = keep.tile([P, PACK, ng * GROUP], BF16, name="gain_raw_%d_%d" % (kp, g0))
+            src = gain[kp * GROUP:(kp + 1) * GROUP, g0 * GROUP:(g0 + ng) * GROUP]
+            nc.sync.dma_start(out=t[:], in_=src.rearrange("(p j) n -> p j n", j=PACK))
+            for g in range(ng):
+                gain_raw[kp, g0 + g] = t[:, :, g * GROUP:(g + 1) * GROUP]
+
+        def load_x(c):
+            for src, dst, nm in ((x, x_raw, "x"), (x_ref, xr_raw, "xr")):
+                t = work.tile([P, B, S], BF16, name=nm, bufs=C)
+                nc.sync.dma_start(out=t[:], in_=src[c * ROWS:(c + 1) * ROWS, :].rearrange("(p b) k -> p b k", b=B))
+                dst[c] = t
+
+        def load_u(c, g0, ng):
+            t = keep.tile([P, B, ng * GROUP], BF16, name="u_raw_%d_%d" % (c, g0))
+            src = u_ref[c * ROWS:(c + 1) * ROWS, g0 * GROUP:(g0 + ng) * GROUP]
+            nc.sync.dma_start(out=t[:], in_=src.rearrange("(p b) n -> p b n", b=B))
+            for g in range(ng):
+                u_raw[c, g0 + g] = t[:, :, g * GROUP:(g + 1) * GROUP]
+
+        def gain_interleave(eng, kp, g):
+            t = work.tile([P, GROUP * PACK], BF16, name="gain_il", align_bytes=64, bufs=3)
+            dst = t[:].rearrange("p (t m j) -> p m j t", t=PACK, j=PACK)
+            src = gain_raw[kp, g].rearrange("p j (m t) -> p m j t", t=PACK)
+            copy(eng, dst, src)
+            gain_il[kp, g] = t
+
+        def gain_quantize(kp, g):
+            cols = slice(g * GROUP, (g + 1) * GROUP)
+            nc.vector.quantize_mx(out=gain_codes[:, kp, cols].bitcast(FP8X4), scales=gain_scales[:, kp, cols],
+                                  in_=gain_il[kp, g][:])
+
+        def err_sub(c, kp):
+            t = work.tile([P, B, GROUP], BF16, name="err", bufs=2)
+            cols = slice(kp * GROUP, (kp + 1) * GROUP)
+            nc.vector.tensor_tensor(out=t[:], in0=xr_raw[c][:, :, cols], in1=x_raw[c][:, :, cols], op=ALU.subtract)
+            err[c, kp] = t
+
+        def turn_words(src, b_of):
+            ps = psum.tile([P, 2, B, P], F32, name="turn", bufs=TURN_BANKS)
+            for b in range(B):
+                words = b_of(src, b).bitcast(F32)
+                for u in range(2):
+                    nc.tensor.transpose(ps[:, u, b, :], words[:, u::2], ident[:])
+            return ps
+
+        def err_turn(c, kp):
+            err_ps[c, kp] = turn_words(err[c, kp], lambda t, b: t[:, b, :])
+
+        def err_copy(eng, c, kp):
+            t = work.tile([P, ROWS * PACK], BF16, name="err_t", align_bytes=64, bufs=2)
+            copy(eng, t[:].bitcast(F32).rearrange("p (r b u) -> p r b u", b=B, u=2),
+                 err_ps[c, kp][:].rearrange("p u b r -> p r b u"))
+            err_t[c, kp] = t
+
+        def err_quantize(c, kp):
+            cols = slice(c * ROWS, (c + 1) * ROWS)
+            nc.vector.quantize_mx(out=err_codes[:, kp, cols].bitcast(FP8X4), scales=err_scales[:, kp, cols],
+                                  in_=err_t[c, kp][:])
+
+        def u_turn(c, g):
+            u_ps[c, g] = turn_words(u_raw[c, g], lambda t, b: t[:, b, :])
+
+        def u_copy(eng, c, g):
+            t = work.tile([P, 2, ROWS * 2], BF16, name="u_t", bufs=4)
+            copy(eng, t[:].bitcast(F32).rearrange("p u (r b) -> p u r b", b=B),
+                 u_ps[c, g][:].rearrange("p u b r -> p u r b"))
+            u_t[c, g] = t
+
+        def multiply(c, g, u):
+            rows = slice(c * ROWS, (c + 1) * ROWS)
+            if True:
+                ps = psum.tile([P, 2, ROWS], F32, name="fb", bufs=FB_BANKS)
+                for e in range(2):
+                    t0 = g * GROUP + (2 * u + e) * P
+                    for kp in range(KP):
+                        nc.tensor.matmul_mx(
+                            out=ps[:, e, :],
+                            lhsT=gain_codes[:, kp, t0:t0 + P].bitcast(FP8X4),
+                            lhsT_scale=gain_scales[:, kp, t0:t0 + P],
+                            rhs=err_codes[:, kp, rows].bitcast(FP8X4),
+                            rhs_scale=err_scales[:, kp, rows],
+                            start=(kp == 0), stop=(kp == KP - 1))
+                fb[c, g, u] = ps
+
+        def add_u(c, g, u):
+            if u == 0:
+                y_t[c, g] = work.tile([P, PACK, ROWS], F32, name="y_t", bufs=3)
+            nc.vector.tensor_tensor(out=y_t[c, g][:, 2 * u:2 * u + 2, :], in0=fb[c, g, u][:],
+                                    in1=u_t[c, g][:, u, :].rearrange("p (m e) -> p e m", e=2), op=ALU.add)
+
+        def clamp(eng, c, g, u):
+            for t in (2 * u, 2 * u + 1):
+                v = y_t[c, g][:, t, :]
+                e = nc.vector if eng == "V" else nc.gpsimd
+                e.tensor_scalar(out=v, in0=v, scalar1=lim[:, 1, g, t:t + 1], scalar2=lim[:, 0, g, t:t + 1],
+                                op0=ALU.min, op1=ALU.max)
+
+        def y_interleave(eng, c, g):
+            y_il[c, g] = work.tile([P, ROWS * PACK], BF16, name="y_il", align_bytes=64, bufs=3)
+            dst = y_il[c, g][:].rearrange("p (c i t) -> p c t i", i=2, t=PACK)
+            copy(eng, dst, y_t[c, g][:].rearrange("p t (c i) -> p c t i", i=2))
+
+        def y_quantize(c, g):
+            if g % 2 == 0:
+                y_codes[c, g // 2] = work.tile([P, 2, ROWS], U32, name="y_codes", align_bytes=64, bufs=4)
+            rows = slice(c * ROWS, (c + 1) * ROWS)
+            plane = last_scales[:, g, :] if c == C - 1 else early_scales[:, g, rows]
+            nc.vector.quantize_mx(out=y_codes[c, g // 2][:, g % 2, :].bitcast(FP8X4), scales=plane,
+                                  in_=y_il[c, g][:])
+
+        def store_codes(c, g):
+            rows = slice(c * ROWS, (c + 1) * ROWS)
+            dst = out_1[g - 1:g + 1, :, rows, :].rearrange("g p m t -> p g (m t)")
+            nc.sync.dma_start(out=dst.bitcast(I32), in_=y_codes[c, g // 2][:].bitcast(I32))
+
+        def y_turn(c, g, b):
+            ps = psum.tile([P, PACK, P], F32, name="back", bufs=BACK_BANKS)
+            for t in range(PACK):
+                nc.tensor.transpose(ps[:, t, :], y_t[c, g][:, t, b * P:(b + 1) * P], ident[:])
+            y_ps[c, g, b] = ps
+
+        def y_copy(eng, c, g, b):
+            if g % 2 == 0 and b == 0:
+                y_rows[c, g // 2] = work.tile([P, B, 2 * GROUP], F32, name="y_rows", bufs=5)
+            t = y_rows[c, g // 2]
+            dst = t[:, b, (g % 2) * GROUP:(g % 2 + 1) * GROUP].rearrange("m (p t) -> m p t", t=PACK)
+            copy(eng, dst, y_ps[c, g, b][:].rearrange("m t p -> m p t"))
+
+        def store_y(c, g, b):
+            t = y_rows[c, g // 2]
+            r0 = c * ROWS + b * P
+            if c == C - 1 and g >= 2:
+                cols = slice((g % 2) * GROUP, (g % 2 + 1) * GROUP)
+                nc.sync.dma_start(out=out_0[r0:r0 + P, g * GROUP:(g + 1) * GROUP], in_=t[:, b, cols])
+            else:
+                nc.sync.dma_start(out=out_0[r0:r0 + P, (g - 1) * GROUP:(g + 1) * GROUP], in_=t[:, b, :])
+
+        def store_scales(plane, m0, m1):
+            for q in range(4):
+                dst = out_2[:, 4 * q:4 * q + 4, m0:m1].rearrange("g r m -> r g m")
+                nc.sync.dma_start(out=dst.bitcast(I32), in_=plane[32 * q:32 * q + 4, :, :].bitcast(I32))
+
+        nc.scalar.dma_start(out=lim_raw[:, 0, :, :], in_=u_lo.rearrange("(g p t) -> p g t", p=P, t=PACK))
+        nc.scalar.dma_start(out=lim_raw[:, 1, :, :], in_=u_hi.rearrange("(g p t) -> p g t", p=P, t=PACK))
+        make_identity(nc, ident[:])
+        nc.gpsimd.tensor_copy(out=lim[:], in_=lim_raw[:])
+
+        def store_planes(last):
+            if last:
+                store_scales(last_scales, M - ROWS, M)
+            else:
+                store_scales(early_scales, 0, M - ROWS)
+
+        fixed = {"lg": load_gain, "lx": load_x, "lu": load_u, "gq": gain_quantize, "sub": err_sub, "et": err_turn,
+                 "eq": err_quantize, "ut": u_turn, "mm": multiply, "add": add_u, "yq": y_quantize, "yt": y_turn,
+                 "sy": store_y, "sc": store_codes, "ss": store_planes}
+        either = {"gi": gain_interleave, "ec": err_copy, "uc": u_copy, "cl": clamp, "yi": y_interleave, "yc": y_copy}
+        for item in ORDER.split():
+            name, digits = item.split(":")
+            args = [int(d) for d in digits if d in "0123456789"]
+            if name in fixed:
+                fixed[name](*args)
+            else:
+                either[name](digits[0], *args)

@@ -22,29 +22,36 @@ G = N // GROUP
 ROWS = 256
 B = ROWS // P
 C = M // ROWS
-FB_BANKS, BACK_BANKS, TURN_BANKS = 3, 3, 2
+BANKS = 8
+
+UNITS = [(0, 1, 0), (0, 1, 1), (1, 1, 0), (1, 1, 1), (0, 2, 2), (0, 2, 3), (2, 2, 0), (2, 2, 1), (2, 1, 2),
+         (2, 1, 3), (3, 1, 2), (3, 1, 3)]
+ERR_SPAN = {0: (0, 1), 1: (1, 1), 2: (2, 2), 3: (2, 2)}
+SCALE_SETS = [(0, 2, 0, 4), (2, 4, 0, 2), (3, 4, 2, 4), (2, 3, 2, 4)]
+
 ORDER = """
-lg:001 lg:101 lx:0 lu:002 lg:111 lg:011 lx:1 lu:102 lg:022 lg:122 lu:022 lu:122 lx:2 lu:204 lx:3 lu:304 gi:S00
-gi:V10 gq:00 gq:10 sub:00 sub:01 et:00 et:01 ec:S00 ec:S01 gi:V11 ut:00 ut:01 uc:S00 eq:00 eq:01 gi:S01 gq:11
-mm:000 uc:V01 mm:001 add:000 sub:11 sub:10 et:11 gq:01 et:10 add:001 ec:S11 mm:010 cl:V000 ec:S10 cl:V001
-mm:011 eq:11 eq:10 yi:S00 ut:10 add:010 yt:000 gi:V02 yt:001 uc:S10 ut:11 yc:S000 mm:100 add:011 uc:S11 mm:101
-yq:00 yc:S001 cl:V010 mm:110 cl:V011 gi:S12 add:100 ut:02 yi:V01 yt:010 yt:011 add:101 ut:03 gq:02 mm:111
-yc:S010 gq:12 yc:S011 sy:010 yq:01 uc:S02 cl:V100 mm:020 sy:011 sc:01 cl:V101 gi:S13 add:110 ut:12 yi:V10
-yt:100 yt:101 add:111 mm:021 gi:V03 yc:S100 mm:120 uc:S03 gq:13 yc:S101 ut:13 gq:03 uc:S12 yq:10 cl:V110
-uc:S13 ut:20 cl:V111 add:020 ut:21 yi:S11 sub:21 yt:110 yt:111 add:021 mm:030 yc:S110 yq:11 yc:S111 mm:031
-cl:V020 sy:110 sc:11 cl:V021 uc:S20 sub:20 sy:111 yt:020 yi:S02 add:030 yt:021 et:21 add:120 yc:S020 add:031
-mm:121 ec:S21 yq:02 cl:V030 mm:130 yc:S021 cl:V031 eq:21 mm:131 uc:S21 yi:V03 yt:030 et:20 add:121 yc:S030
-yt:031 yq:03 cl:V120 ut:22 ec:S20 sc:03 sy:030 cl:V121 yc:S031 add:130 yt:120 eq:20 yi:S12 yt:121 sy:031
-add:131 ut:23 cl:V130 mm:200 yc:S120 cl:V131 yq:12 mm:201 uc:S22 yi:V13 mm:210 yc:S121 add:200 yt:130 uc:S23
-yq:13 yt:131 add:201 yc:S130 mm:211 sc:13 cl:V200 yc:S131 ut:30 cl:V201 sy:130 sub:31 mm:220 yi:S20 sy:131
-sub:30 yt:200 add:210 yt:201 uc:S30 et:30 yq:20 yc:S200 add:211 mm:221 ec:S30 cl:V210 et:31 cl:V211 yc:S201
-add:220 yt:210 yi:S21 eq:30 yt:211 add:221 ut:31 cl:V220 mm:230 ec:S31 cl:V221 yq:21 yc:S210 mm:231 eq:31
-yc:S211 sc:21 yt:220 yi:V22 sy:210 yt:221 uc:S31 add:230 ut:32 sy:211 yc:S220 yq:22 mm:300 add:231 uc:S32
-mm:301 cl:V230 yc:S221 cl:V231 mm:310 add:300 yi:S23 yt:230 add:310 yt:231 ut:33 add:301 yc:S230 mm:311 yq:23
-yc:S231 cl:V300 sy:230 mm:320 sc:23 cl:V301 ss:0 uc:S33 add:311 mm:321 sy:231 yi:S30 cl:V310 yt:300 cl:V311
-yt:301 add:320 mm:330 yc:S300 yi:V31 mm:331 yc:S301 yq:30 yt:310 add:321 yt:311 yq:31 yc:S310 cl:V320 sc:31
-cl:V321 yc:S311 sy:310 add:330 yi:S32 yt:320 sy:311 yt:321 add:331 cl:V330 yc:S320 cl:V331 yq:32 yc:S321
-sy:320 yt:330 yi:V33 yt:331 yc:S330 sy:321 yq:33 yc:S331 sc:33 sy:330 ss:1 sy:331
+lg:102 lx:0 lx:1 lg:002 lu:002 ll: lg:022 pg:V10 pg:S11 lu:102 sub:0 lg:122 qg:10 te:01 qg:11 te:00 lu:022
+lu:122 sub:1 ce:S01 ce:S00 qe:01 te:11 qe:00 pg:V01 pg:S00 lx:2 te:10 tu:01 ce:V10 lx:3 qg:01 tu:00 ce:S11 qg:00
+cu:S01 qe:10 mm:000 qe:11 cu:S00 pg:V02 lu:204 pg:S03 mm:001 add:000 wl: lu:304 qg:02 mm:010 lim:V001 tu:10
+add:001 lim:G000 mm:011 qg:03 cu:S10 add:010 lim:G002 mm:100 pg:S13 lim:G003 add:011 mm:101 pg:V12 mm:111 tu:11
+ty:001 lim:V010 lim:V011 ty:000 cu:S11 add:100 lim:G012 tu:02 lim:V013 py:S00 qg:12 mm:110 cu:V02 lim:G100
+ty:010 py:S01 lim:G101 add:101 tu:03 tu:12 qy:00 add:110 lim:G102 cy:S000 mm:021 lim:G103 add:111 cu:S03 mm:020
+sub:2 cu:S12 ty:011 ty:100 cy:S001 tu:13 lim:V111 cy:S011 qg:13 te:21 mm:023 cy:S010 add:020 lim:G113 ce:S21
+lim:V110 mm:022 sub:3 sy:01202 cy:S100 mm:033 mm:030 cu:S13 add:023 lim:G020 ty:101 py:S10 add:022 te:31
+lim:G112 te:20 add:021 lim:G023 te:30 cy:S101 ce:V31 ty:110 lim:G021 tu:20 ce:S20 add:030 mm:032 ce:S30 qe:21
+mm:031 cu:S20 qy:01 lim:V022 tu:30 cy:S110 sc:012 qe:20 py:S11 ty:021 add:032 lim:G030 ty:111 ty:020 add:033
+mm:200 lim:G032 cy:S020 add:031 mm:203 lim:G033 cy:S021 cy:V111 ty:120 py:S02 lim:V031 tu:21 sy:11202 qy:10
+ty:030 py:V03 ty:031 cu:S30 mm:202 py:V12 cy:S030 qy:11 mm:210 add:200 cy:S031 sc:112 mm:212 qy:02 cu:S21 mm:201
+sy:03202 add:203 lim:G200 py:S13 tu:31 add:202 lim:G203 tu:22 add:201 cu:S31 ty:121 qy:03 ty:131 cy:S120 ty:130
+add:210 lim:G201 mm:213 cy:S131 ss:0 add:212 sc:032 cy:S121 mm:211 lim:G202 add:213 cy:S130 tu:33 lim:G210
+add:211 py:S20 tu:32 sy:13202 lim:V213 ty:300 lim:V211 mm:320 lim:V212 cu:S32 py:V30 ty:310 cy:S300 py:V21
+ty:311 ty:200 cy:S310 py:V31 ty:301 cy:S311 ty:211 qy:20 sy:31201 mm:321 cy:S301 add:320 mm:221 cy:S200 sy:31212
+qy:21 mm:220 cu:S22 add:321 lim:G321 ty:201 cy:S211 ss:1 ty:210 lim:V320 sc:212 lim:G322 cu:S33 tu:23 add:220
+lim:G323 mm:330 cy:S210 cy:V201 lim:G221 cu:S23 add:221 mm:331 lim:G220 sy:21202 py:S32 add:330 ty:321 lim:G222
+ty:320 add:331 lim:G223 mm:230 cy:S320 lim:V331 lim:V330 mm:231 lim:V333 cy:S321 lim:G332 add:230 ty:220
+sy:32101 qy:32 sy:32112 ty:331 add:231 lim:G231 cy:S220 ty:330 sc:321 lim:V230 ty:221 cy:S331 lim:V233 sy:22101
+lim:V232 py:V33 cy:S330 ty:231 sy:33112 ty:230 py:V22 cy:S221 sy:33101 cy:S231 qy:33 sy:22112 qy:22 cy:S230
+py:V23 sy:23112 ss:2 sy:23101 sc:331 qy:23 sc:232 ss:3
 """
 
 
@@ -52,191 +59,217 @@ def tile_saturated_state_feedback_g1_kernel(tc, x, x_ref, gain, u_ref, u_lo, u_h
     nc = tc.nc
     with ExitStack() as ctx:
         keep = ctx.enter_context(tc.tile_pool(name="keep", bufs=1))
-        work = ctx.enter_context(tc.tile_pool(name="work", bufs=3))
-        psum = ctx.enter_context(tc.psum_pool(name="psum", bufs=2))
+        work = ctx.enter_context(tc.tile_pool(name="work", bufs=2))
+        psum = ctx.enter_context(tc.psum_pool(name="psum", bufs=1))
         ctx.enter_context(tc.manual_schedule())
 
         ident = keep.tile([P, P], F32, name="ident")
-        lim_raw = keep.tile([P, 2, G, PACK], BF16, name="lim_raw")
-        lim = keep.tile([P, 2, G, PACK], F32, name="lim")
+        limits_raw = keep.tile([P, 2, G, PACK], BF16, name="limits_raw")
+        limits = keep.tile([P, 2, G, PACK], F32, name="limits")
         gain_codes = keep.tile([P, KP, N], U32, name="gain_codes", align_bytes=64)
         gain_scales = keep.tile([P, KP, N], U8, name="gain_scales", align_bytes=64)
         err_codes = keep.tile([P, KP, M], U32, name="err_codes", align_bytes=64)
         err_scales = keep.tile([P, KP, M], U8, name="err_scales", align_bytes=64)
-        early_scales = keep.tile([P, G, M - ROWS], U8, name="early_scales", align_bytes=64)
-        last_scales = keep.tile([P, G, ROWS], U8, name="last_scales", align_bytes=64)
+        y_scales = [keep.tile([P, g1 - g0, (c1 - c0) * ROWS], U8, name="y_scales_%d_%d" % (c0, g0), align_bytes=64)
+                    for c0, c1, g0, g1 in SCALE_SETS]
+        scale_set_of = {(c, g): i for i, (c0, c1, g0, g1) in enumerate(SCALE_SETS)
+                        for c in range(c0, c1) for g in range(g0, g1)}
+        unit_of = {(c, g): (c0, w) for c0, w, g in UNITS for c in range(c0, c0 + w)}
 
-        gain_raw, x_raw, xr_raw, u_raw = {}, {}, {}, {}
-        gain_il, err, err_t, err_ps, u_ps, u_t, fb, y_t, y_il, y_ps, y_rows, y_codes = ({} for k in range(12))
+        gain_raw, x_raw, x_ref_raw, u_raw = {}, {}, {}, {}
+        gain_packed, err, err_packed, u_turned, y_turned, y_packed, y_rows, y_codes = ({} for k in range(8))
 
-        def copy(eng, dst, src):
-            if eng == "V":
+        free_banks = list(range(BANKS))
+        filled = {}
+
+        def take_bank(key, shape):
+            bank = free_banks[0]
+            free_banks.remove(bank)
+            tile = psum.tile(shape, F32, name="bank_%d" % bank)
+            filled[key] = (bank, tile)
+            return tile
+
+        def empty_bank(key):
+            bank, tile = filled[key]
+            free_banks.append(bank)
+            return tile
+
+        def copy(engine, dst, src):
+            if engine == "V":
                 nc.vector.tensor_copy(out=dst, in_=src)
             else:
                 nc.scalar.copy(out=dst, in_=src)
 
-        def load_gain(kp, g0, ng):
-            t = keep.tile([P, PACK, ng * GROUP], BF16, name="gain_raw_%d_%d" % (kp, g0))
-            src = gain[kp * GROUP:(kp + 1) * GROUP, g0 * GROUP:(g0 + ng) * GROUP]
-            nc.sync.dma_start(out=t[:], in_=src.rearrange("(p j) n -> p j n", j=PACK))
-            for g in range(ng):
-                gain_raw[kp, g0 + g] = t[:, :, g * GROUP:(g + 1) * GROUP]
+        def load_limits():
+            nc.sync.dma_start(out=limits_raw[:, 0, :, :], in_=u_lo.rearrange("(g p t) -> p g t", p=P, t=PACK))
+            nc.sync.dma_start(out=limits_raw[:, 1, :, :], in_=u_hi.rearrange("(g p t) -> p g t", p=P, t=PACK))
 
-        def load_x(c):
-            for src, dst, nm in ((x, x_raw, "x"), (x_ref, xr_raw, "xr")):
-                t = work.tile([P, B, S], BF16, name=nm, bufs=C)
-                nc.sync.dma_start(out=t[:], in_=src[c * ROWS:(c + 1) * ROWS, :].rearrange("(p b) k -> p b k", b=B))
-                dst[c] = t
+        def widen_limits():
+            nc.gpsimd.tensor_copy(out=limits[:], in_=limits_raw[:])
 
-        def load_u(c, g0, ng):
-            t = keep.tile([P, B, ng * GROUP], BF16, name="u_raw_%d_%d" % (c, g0))
-            src = u_ref[c * ROWS:(c + 1) * ROWS, g0 * GROUP:(g0 + ng) * GROUP]
-            nc.sync.dma_start(out=t[:], in_=src.rearrange("(p b) n -> p b n", b=B))
-            for g in range(ng):
-                u_raw[c, g0 + g] = t[:, :, g * GROUP:(g + 1) * GROUP]
+        def load_gain(kp, g0, count):
+            tile = keep.tile([P, PACK, count * GROUP], BF16, name="gain_raw_%d_%d" % (kp, g0))
+            src = gain[kp * GROUP:(kp + 1) * GROUP, g0 * GROUP:(g0 + count) * GROUP]
+            nc.sync.dma_start(out=tile[:], in_=src.rearrange("(p j) n -> p j n", j=PACK))
+            for g in range(count):
+                gain_raw[kp, g0 + g] = tile[:, :, g * GROUP:(g + 1) * GROUP]
 
-        def gain_interleave(eng, kp, g):
-            t = work.tile([P, GROUP * PACK], BF16, name="gain_il", align_bytes=64, bufs=3)
-            dst = t[:].rearrange("p (t m j) -> p m j t", t=PACK, j=PACK)
-            src = gain_raw[kp, g].rearrange("p j (m t) -> p m j t", t=PACK)
-            copy(eng, dst, src)
-            gain_il[kp, g] = t
+        def load_states(c):
+            for src, tiles, name in ((x, x_raw, "x_raw"), (x_ref, x_ref_raw, "x_ref_raw")):
+                tiles[c] = work.tile([P, B, S], BF16, name=name, bufs=2)
+                rows = src[c * ROWS:(c + 1) * ROWS, :]
+                nc.sync.dma_start(out=tiles[c][:], in_=rows.rearrange("(r b) k -> r b k", b=B))
 
-        def gain_quantize(kp, g):
+        def load_u(c, g0, count):
+            tile = keep.tile([P, B, count * GROUP], BF16, name="u_raw_%d_%d" % (c, g0))
+            src = u_ref[c * ROWS:(c + 1) * ROWS, g0 * GROUP:(g0 + count) * GROUP]
+            nc.sync.dma_start(out=tile[:], in_=src.rearrange("(r b) n -> r b n", b=B))
+            for g in range(count):
+                u_raw[c, g0 + g] = tile[:, :, g * GROUP:(g + 1) * GROUP]
+
+        def pack_gain(engine, kp, g):
+            gain_packed[kp, g] = work.tile([P, PACK, P, PACK], BF16, name="gain_packed", align_bytes=64, bufs=2)
+            copy(engine, gain_packed[kp, g][:].rearrange("p t m j -> p m j t"),
+                 gain_raw[kp, g].rearrange("p j (m t) -> p m j t", t=PACK))
+
+        def quantize_gain(kp, g):
             cols = slice(g * GROUP, (g + 1) * GROUP)
             nc.vector.quantize_mx(out=gain_codes[:, kp, cols].bitcast(FP8X4), scales=gain_scales[:, kp, cols],
-                                  in_=gain_il[kp, g][:])
+                                  in_=gain_packed[kp, g][:].rearrange("p t m j -> p (t m j)"))
 
-        def err_sub(c, kp):
-            t = work.tile([P, B, GROUP], BF16, name="err", bufs=2)
-            cols = slice(kp * GROUP, (kp + 1) * GROUP)
-            nc.vector.tensor_tensor(out=t[:], in0=xr_raw[c][:, :, cols], in1=x_raw[c][:, :, cols], op=ALU.subtract)
-            err[c, kp] = t
+        def subtract(c):
+            err[c] = work.tile([P, 2, B * S // 2], BF16, name="err", bufs=2)
+            pairs = "r b (q u e) -> r u (b q) e"
+            nc.vector.tensor_tensor(out=err[c][:].rearrange("r u (q e) -> r u q e", e=2),
+                                    in0=x_ref_raw[c][:].rearrange(pairs, u=2, e=2),
+                                    in1=x_raw[c][:].rearrange(pairs, u=2, e=2), op=ALU.subtract)
 
-        def turn_words(src, b_of):
-            ps = psum.tile([P, 2, B, P], F32, name="turn", bufs=TURN_BANKS)
-            for b in range(B):
-                words = b_of(src, b).bitcast(F32)
-                for u in range(2):
-                    nc.tensor.transpose(ps[:, u, b, :], words[:, u::2], ident[:])
-            return ps
+        def turn_err(c, kp):
+            bank = take_bank(("err", c, kp), [P, 2, B, P])
+            words = err[c][:].bitcast(F32)
+            for u in range(2):
+                for b in range(B):
+                    q0 = (b * KP + kp) * P
+                    nc.tensor.transpose(bank[:, u, b, :], words[:, u, q0:q0 + P], ident[:])
 
-        def err_turn(c, kp):
-            err_ps[c, kp] = turn_words(err[c, kp], lambda t, b: t[:, b, :])
+        def copy_err(engine, c, kp):
+            c0, w = ERR_SPAN[c]
+            if c == c0:
+                err_packed[c0, kp] = work.tile([P, w * ROWS * PACK], BF16, name="err_packed", align_bytes=64,
+                                               bufs=2)
+            dst = err_packed[c0, kp][:, (c - c0) * ROWS * PACK:(c - c0 + 1) * ROWS * PACK]
+            copy(engine, dst.bitcast(F32).rearrange("p (r b u) -> p r b u", b=B, u=2),
+                 empty_bank(("err", c, kp))[:].rearrange("p u b r -> p r b u"))
 
-        def err_copy(eng, c, kp):
-            t = work.tile([P, ROWS * PACK], BF16, name="err_t", align_bytes=64, bufs=2)
-            copy(eng, t[:].bitcast(F32).rearrange("p (r b u) -> p r b u", b=B, u=2),
-                 err_ps[c, kp][:].rearrange("p u b r -> p r b u"))
-            err_t[c, kp] = t
-
-        def err_quantize(c, kp):
-            cols = slice(c * ROWS, (c + 1) * ROWS)
+        def quantize_err(c, kp):
+            cols = slice(c * ROWS, (c + ERR_SPAN[c][1]) * ROWS)
             nc.vector.quantize_mx(out=err_codes[:, kp, cols].bitcast(FP8X4), scales=err_scales[:, kp, cols],
-                                  in_=err_t[c, kp][:])
+                                  in_=err_packed[c, kp][:])
 
-        def u_turn(c, g):
-            u_ps[c, g] = turn_words(u_raw[c, g], lambda t, b: t[:, b, :])
+        def turn_u(c, g):
+            bank = take_bank(("u", c, g), [P, 2, B, P])
+            for b in range(B):
+                words = u_raw[c, g][:, b, :].bitcast(F32)
+                for u in range(2):
+                    nc.tensor.transpose(bank[:, u, b, :], words[:, u::2], ident[:])
 
-        def u_copy(eng, c, g):
-            t = work.tile([P, 2, ROWS * 2], BF16, name="u_t", bufs=4)
-            copy(eng, t[:].bitcast(F32).rearrange("p u (r b) -> p u r b", b=B),
-                 u_ps[c, g][:].rearrange("p u b r -> p u r b"))
-            u_t[c, g] = t
+        def copy_u(engine, c, g):
+            c0, w = unit_of[c, g]
+            if c == c0:
+                u_turned[c0, g] = work.tile([P, 2, w * ROWS * 2], BF16, name="u_turned", bufs=3)
+            dst = u_turned[c0, g][:, :, (c - c0) * ROWS * 2:(c - c0 + 1) * ROWS * 2]
+            copy(engine, dst.bitcast(F32).rearrange("p u (r b) -> p u r b", b=B),
+                 empty_bank(("u", c, g))[:].rearrange("p u b r -> p u r b"))
 
-        def multiply(c, g, u):
-            rows = slice(c * ROWS, (c + 1) * ROWS)
-            if True:
-                ps = psum.tile([P, 2, ROWS], F32, name="fb", bufs=FB_BANKS)
-                for e in range(2):
-                    t0 = g * GROUP + (2 * u + e) * P
-                    for kp in range(KP):
-                        nc.tensor.matmul_mx(
-                            out=ps[:, e, :],
-                            lhsT=gain_codes[:, kp, t0:t0 + P].bitcast(FP8X4),
-                            lhsT_scale=gain_scales[:, kp, t0:t0 + P],
-                            rhs=err_codes[:, kp, rows].bitcast(FP8X4),
-                            rhs_scale=err_scales[:, kp, rows],
-                            start=(kp == 0), stop=(kp == KP - 1))
-                fb[c, g, u] = ps
+        def multiply(c, g, i):
+            w = unit_of[c, g][1]
+            slots = 2 // w
+            rows = slice(c * ROWS, (c + w) * ROWS)
+            bank = take_bank(("fb", c, g, i), [P, slots, w * ROWS])
+            for e in range(slots):
+                n0 = g * GROUP + (slots * i + e) * P
+                for kp in range(KP):
+                    nc.tensor.matmul_mx(
+                        out=bank[:, e, :],
+                        lhsT=gain_codes[:, kp, n0:n0 + P].bitcast(FP8X4),
+                        lhsT_scale=gain_scales[:, kp, n0:n0 + P],
+                        rhs=err_codes[:, kp, rows].bitcast(FP8X4),
+                        rhs_scale=err_scales[:, kp, rows],
+                        start=(kp == 0), stop=(kp == KP - 1))
 
-        def add_u(c, g, u):
-            if u == 0:
-                y_t[c, g] = work.tile([P, PACK, ROWS], F32, name="y_t", bufs=3)
-            nc.vector.tensor_tensor(out=y_t[c, g][:, 2 * u:2 * u + 2, :], in0=fb[c, g, u][:],
-                                    in1=u_t[c, g][:, u, :].rearrange("p (m e) -> p e m", e=2), op=ALU.add)
+        def add_u(c, g, i):
+            w = unit_of[c, g][1]
+            slots = 2 // w
+            if i == 0:
+                y_turned[c, g] = work.tile([P, PACK, w * ROWS], F32, name="y_turned", bufs=3)
+            t0 = slots * i
+            u_pair = u_turned[c, g][:, t0 // 2, :].rearrange("p (m e) -> p e m", e=2)
+            nc.vector.tensor_tensor(out=y_turned[c, g][:, t0:t0 + slots, :], in0=empty_bank(("fb", c, g, i))[:],
+                                    in1=u_pair[:, t0 % 2:t0 % 2 + slots, :], op=ALU.add)
 
-        def clamp(eng, c, g, u):
-            for t in (2 * u, 2 * u + 1):
-                v = y_t[c, g][:, t, :]
-                e = nc.vector if eng == "V" else nc.gpsimd
-                e.tensor_scalar(out=v, in0=v, scalar1=lim[:, 1, g, t:t + 1], scalar2=lim[:, 0, g, t:t + 1],
-                                op0=ALU.min, op1=ALU.max)
+        def limit(engine, c, g, t):
+            values = y_turned[c, g][:, t, :]
+            builder = nc.vector if engine == "V" else nc.gpsimd
+            builder.tensor_scalar(out=values, in0=values, scalar1=limits[:, 1, g, t:t + 1],
+                                  scalar2=limits[:, 0, g, t:t + 1], op0=ALU.min, op1=ALU.max)
 
-        def y_interleave(eng, c, g):
-            y_il[c, g] = work.tile([P, ROWS * PACK], BF16, name="y_il", align_bytes=64, bufs=3)
-            dst = y_il[c, g][:].rearrange("p (c i t) -> p c t i", i=2, t=PACK)
-            copy(eng, dst, y_t[c, g][:].rearrange("p t (c i) -> p c t i", i=2))
+        def pack_y(engine, c, g):
+            c0, w = unit_of[c, g]
+            if c == c0:
+                y_packed[c0, g] = work.tile([P, w * ROWS * PACK], BF16, name="y_packed", align_bytes=64, bufs=3)
+            m0 = (c - c0) * ROWS
+            dst = y_packed[c0, g][:, m0 * PACK:(m0 + ROWS) * PACK].rearrange("p (m i t) -> p m t i", i=2, t=PACK)
+            copy(engine, dst, y_turned[c0, g][:, :, m0:m0 + ROWS].rearrange("p t (m i) -> p m t i", i=2))
 
-        def y_quantize(c, g):
+        def quantize_y(c, g):
+            w = unit_of[c, g][1]
             if g % 2 == 0:
-                y_codes[c, g // 2] = work.tile([P, 2, ROWS], U32, name="y_codes", align_bytes=64, bufs=4)
-            rows = slice(c * ROWS, (c + 1) * ROWS)
-            plane = last_scales[:, g, :] if c == C - 1 else early_scales[:, g, rows]
-            nc.vector.quantize_mx(out=y_codes[c, g // 2][:, g % 2, :].bitcast(FP8X4), scales=plane,
-                                  in_=y_il[c, g][:])
+                y_codes[c, g // 2] = work.tile([P, 2, w * ROWS], U32, name="y_codes", align_bytes=64, bufs=3)
+            i = scale_set_of[c, g]
+            m0 = (c - SCALE_SETS[i][0]) * ROWS
+            nc.vector.quantize_mx(out=y_codes[c, g // 2][:, g % 2, :].bitcast(FP8X4),
+                                  scales=y_scales[i][:, g - SCALE_SETS[i][2], m0:m0 + w * ROWS], in_=y_packed[c, g][:])
 
-        def store_codes(c, g):
-            rows = slice(c * ROWS, (c + 1) * ROWS)
-            dst = out_1[g - 1:g + 1, :, rows, :].rearrange("g p m t -> p g (m t)")
-            nc.sync.dma_start(out=dst.bitcast(I32), in_=y_codes[c, g // 2][:].bitcast(I32))
-
-        def y_turn(c, g, b):
-            ps = psum.tile([P, PACK, P], F32, name="back", bufs=BACK_BANKS)
+        def turn_y(c, g, b):
+            bank = take_bank(("y", c, g, b), [P, PACK, P])
+            c0 = unit_of[c, g][0]
+            m0 = (c - c0) * ROWS + b * P
             for t in range(PACK):
-                nc.tensor.transpose(ps[:, t, :], y_t[c, g][:, t, b * P:(b + 1) * P], ident[:])
-            y_ps[c, g, b] = ps
+                nc.tensor.transpose(bank[:, t, :], y_turned[c0, g][:, t, m0:m0 + P], ident[:])
 
-        def y_copy(eng, c, g, b):
+        def copy_y(engine, c, g, b):
             if g % 2 == 0 and b == 0:
-                y_rows[c, g // 2] = work.tile([P, B, 2 * GROUP], F32, name="y_rows", bufs=5)
-            t = y_rows[c, g // 2]
-            dst = t[:, b, (g % 2) * GROUP:(g % 2 + 1) * GROUP].rearrange("m (p t) -> m p t", t=PACK)
-            copy(eng, dst, y_ps[c, g, b][:].rearrange("m t p -> m p t"))
+                y_rows[c, g // 2] = work.tile([P, B, 2 * GROUP], F32, name="y_rows", bufs=4)
+            dst = y_rows[c, g // 2][:, b, (g % 2) * GROUP:(g % 2 + 1) * GROUP]
+            copy(engine, dst.rearrange("m (p t) -> m p t", t=PACK),
+                 empty_bank(("y", c, g, b))[:].rearrange("m t p -> m p t"))
 
-        def store_y(c, g, b):
-            t = y_rows[c, g // 2]
-            r0 = c * ROWS + b * P
-            if c == C - 1 and g >= 2:
-                cols = slice((g % 2) * GROUP, (g % 2 + 1) * GROUP)
-                nc.sync.dma_start(out=out_0[r0:r0 + P, g * GROUP:(g + 1) * GROUP], in_=t[:, b, cols])
-            else:
-                nc.sync.dma_start(out=out_0[r0:r0 + P, (g - 1) * GROUP:(g + 1) * GROUP], in_=t[:, b, :])
+        def store_y(c, g, count, b0, b1):
+            src = y_rows[c, g // 2][:, b0:b1, (g % 2 + 1 - count) * GROUP:(g % 2 + 1) * GROUP]
+            dst = out_0[c * ROWS + b0 * P:c * ROWS + b1 * P, (g + 1 - count) * GROUP:(g + 1) * GROUP]
+            nc.sync.dma_start(out=dst.rearrange("(b m) n -> m b n", m=P), in_=src)
 
-        def store_scales(plane, m0, m1):
-            for q in range(4):
-                dst = out_2[:, 4 * q:4 * q + 4, m0:m1].rearrange("g r m -> r g m")
-                nc.sync.dma_start(out=dst.bitcast(I32), in_=plane[32 * q:32 * q + 4, :, :].bitcast(I32))
+        def store_codes(c, g, count):
+            rows = slice(c * ROWS, (c + unit_of[c, g][1]) * ROWS)
+            dst = out_1[g + 1 - count:g + 1, :, rows, :].rearrange("g p m t -> p g (m t)")
+            src = y_codes[c, g // 2][:, g % 2 + 1 - count:g % 2 + 1, :]
+            nc.sync.dma_start(out=dst.bitcast(I32), in_=src.bitcast(I32))
 
-        nc.scalar.dma_start(out=lim_raw[:, 0, :, :], in_=u_lo.rearrange("(g p t) -> p g t", p=P, t=PACK))
-        nc.scalar.dma_start(out=lim_raw[:, 1, :, :], in_=u_hi.rearrange("(g p t) -> p g t", p=P, t=PACK))
+        def store_scales(i):
+            c0, c1, g0, g1 = SCALE_SETS[i]
+            queue = nc.scalar if i == len(SCALE_SETS) - 1 else nc.sync
+            for q in range(P // 32):
+                dst = out_2[g0:g1, 4 * q:4 * q + 4, c0 * ROWS:c1 * ROWS].rearrange("g r m -> r g m")
+                queue.dma_start(out=dst.bitcast(I32), in_=y_scales[i][32 * q:32 * q + 4, :, :].bitcast(I32))
+
         make_identity(nc, ident[:])
-        nc.gpsimd.tensor_copy(out=lim[:], in_=lim_raw[:])
 
-        def store_planes(last):
-            if last:
-                store_scales(last_scales, M - ROWS, M)
-            else:
-                store_scales(early_scales, 0, M - ROWS)
-
-        fixed = {"lg": load_gain, "lx": load_x, "lu": load_u, "gq": gain_quantize, "sub": err_sub, "et": err_turn,
-                 "eq": err_quantize, "ut": u_turn, "mm": multiply, "add": add_u, "yq": y_quantize, "yt": y_turn,
-                 "sy": store_y, "sc": store_codes, "ss": store_planes}
-        either = {"gi": gain_interleave, "ec": err_copy, "uc": u_copy, "cl": clamp, "yi": y_interleave, "yc": y_copy}
-        for item in ORDER.split():
-            name, digits = item.split(":")
-            args = [int(d) for d in digits if d in "0123456789"]
-            if name in fixed:
-                fixed[name](*args)
-            else:
-                either[name](digits[0], *args)
+        steps = {"ll": load_limits, "wl": widen_limits, "lg": load_gain, "lx": load_states, "lu": load_u,
+                 "pg": pack_gain, "qg": quantize_gain,
+                 "sub": subtract, "te": turn_err, "ce": copy_err, "qe": quantize_err,
+                 "tu": turn_u, "cu": copy_u, "mm": multiply, "add": add_u, "lim": limit,
+                 "py": pack_y, "qy": quantize_y, "ty": turn_y, "cy": copy_y,
+                 "sy": store_y, "sc": store_codes, "ss": store_scales}
+        for step in ORDER.split():
+            name, args = step.split(":")
+            steps[name](*[a if a in "VSG" else int(a) for a in args])

from contextlib import ExitStack

import concourse.mybir as mybir
from concourse.masks import make_identity

M, S, N = 1024, 1024, 2048
FLOPS = 2 * M * S * N

F32 = mybir.dt.float32
BF16 = mybir.dt.bfloat16
I32 = mybir.dt.int32
U32 = mybir.dt.uint32
U8 = mybir.dt.uint8
FP8X4 = mybir.dt.float8_e4m3fn_x4
ALU = mybir.AluOpType

P = 128
PACK = 4
GROUP = P * PACK
KP = S // GROUP
G = N // GROUP
ROWS = 256
B = ROWS // P
C = M // ROWS
BANKS = 8

UNITS = [(0, 1, 0), (0, 1, 1), (1, 1, 0), (1, 1, 1), (0, 2, 2), (0, 2, 3), (2, 2, 0), (2, 2, 1), (2, 1, 2),
         (2, 1, 3), (3, 1, 2), (3, 1, 3)]
ERR_SPAN = {0: (0, 1), 1: (1, 1), 2: (2, 2), 3: (2, 2)}
SCALE_SETS = [(0, 2, 0, 4), (2, 4, 0, 2), (3, 4, 2, 4), (2, 3, 2, 4)]

ORDER = """
lg:102 lx:0 lx:1 lg:002 lu:002 ll: lg:022 pg:V10 pg:S11 lu:102 sub:0 lg:122 qg:10 te:01 qg:11 te:00 lu:022
lu:122 sub:1 ce:S01 ce:S00 qe:01 te:11 qe:00 pg:V01 pg:S00 lx:2 te:10 tu:01 ce:V10 lx:3 qg:01 tu:00 ce:S11 qg:00
cu:S01 qe:10 mm:000 qe:11 cu:S00 pg:V02 lu:204 pg:S03 mm:001 add:000 wl: lu:304 qg:02 mm:010 lim:V001 tu:10
add:001 lim:G000 mm:011 qg:03 cu:S10 add:010 lim:G002 mm:100 pg:S13 lim:G003 add:011 mm:101 pg:V12 mm:111 tu:11
ty:001 lim:V010 lim:V011 ty:000 cu:S11 add:100 lim:G012 tu:02 lim:V013 py:S00 qg:12 mm:110 cu:V02 lim:G100
ty:010 py:S01 lim:G101 add:101 tu:03 tu:12 qy:00 add:110 lim:G102 cy:S000 mm:021 lim:G103 add:111 cu:S03 mm:020
sub:2 cu:S12 ty:011 ty:100 cy:S001 tu:13 lim:V111 cy:S011 qg:13 te:21 mm:023 cy:S010 add:020 lim:G113 ce:S21
lim:V110 mm:022 sub:3 sy:01202 cy:S100 mm:033 mm:030 cu:S13 add:023 lim:G020 ty:101 py:S10 add:022 te:31
lim:G112 te:20 add:021 lim:G023 te:30 cy:S101 ce:V31 ty:110 lim:G021 tu:20 ce:S20 add:030 mm:032 ce:S30 qe:21
mm:031 cu:S20 qy:01 lim:V022 tu:30 cy:S110 sc:012 qe:20 py:S11 ty:021 add:032 lim:G030 ty:111 ty:020 add:033
mm:200 lim:G032 cy:S020 add:031 mm:203 lim:G033 cy:S021 cy:V111 ty:120 py:S02 lim:V031 tu:21 sy:11202 qy:10
ty:030 py:V03 ty:031 cu:S30 mm:202 py:V12 cy:S030 qy:11 mm:210 add:200 cy:S031 sc:112 mm:212 qy:02 cu:S21 mm:201
sy:03202 add:203 lim:G200 py:S13 tu:31 add:202 lim:G203 tu:22 add:201 cu:S31 ty:121 qy:03 ty:131 cy:S120 ty:130
add:210 lim:G201 mm:213 cy:S131 ss:0 add:212 sc:032 cy:S121 mm:211 lim:G202 add:213 cy:S130 tu:33 lim:G210
add:211 py:S20 tu:32 sy:13202 lim:V213 ty:300 lim:V211 mm:320 lim:V212 cu:S32 py:V30 ty:310 cy:S300 py:V21
ty:311 ty:200 cy:S310 py:V31 ty:301 cy:S311 ty:211 qy:20 sy:31201 mm:321 cy:S301 add:320 mm:221 cy:S200 sy:31212
qy:21 mm:220 cu:S22 add:321 lim:G321 ty:201 cy:S211 ss:1 ty:210 lim:V320 sc:212 lim:G322 cu:S33 tu:23 add:220
lim:G323 mm:330 cy:S210 cy:V201 lim:G221 cu:S23 add:221 mm:331 lim:G220 sy:21202 py:S32 add:330 ty:321 lim:G222
ty:320 add:331 lim:G223 mm:230 cy:S320 lim:V331 lim:V330 mm:231 lim:V333 cy:S321 lim:G332 add:230 ty:220
sy:32101 qy:32 sy:32112 ty:331 add:231 lim:G231 cy:S220 ty:330 sc:321 lim:V230 ty:221 cy:S331 lim:V233 sy:22101
lim:V232 py:V33 cy:S330 ty:231 sy:33112 ty:230 py:V22 cy:S221 sy:33101 cy:S231 qy:33 sy:22112 qy:22 cy:S230
py:V23 sy:23112 ss:2 sy:23101 sc:331 qy:23 sc:232 ss:3
"""


def tile_saturated_state_feedback_g1_kernel(tc, x, x_ref, gain, u_ref, u_lo, u_hi, out_0, out_1, out_2):
    nc = tc.nc
    with ExitStack() as ctx:
        keep = ctx.enter_context(tc.tile_pool(name="keep", bufs=1))
        work = ctx.enter_context(tc.tile_pool(name="work", bufs=2))
        psum = ctx.enter_context(tc.psum_pool(name="psum", bufs=1))
        ctx.enter_context(tc.manual_schedule())

        ident = keep.tile([P, P], F32, name="ident")
        limits_raw = keep.tile([P, 2, G, PACK], BF16, name="limits_raw")
        limits = keep.tile([P, 2, G, PACK], F32, name="limits")
        gain_codes = keep.tile([P, KP, N], U32, name="gain_codes", align_bytes=64)
        gain_scales = keep.tile([P, KP, N], U8, name="gain_scales", align_bytes=64)
        err_codes = keep.tile([P, KP, M], U32, name="err_codes", align_bytes=64)
        err_scales = keep.tile([P, KP, M], U8, name="err_scales", align_bytes=64)
        y_scales = [keep.tile([P, g1 - g0, (c1 - c0) * ROWS], U8, name="y_scales_%d_%d" % (c0, g0), align_bytes=64)
                    for c0, c1, g0, g1 in SCALE_SETS]
        scale_set_of = {(c, g): i for i, (c0, c1, g0, g1) in enumerate(SCALE_SETS)
                        for c in range(c0, c1) for g in range(g0, g1)}
        unit_of = {(c, g): (c0, w) for c0, w, g in UNITS for c in range(c0, c0 + w)}

        gain_raw, x_raw, x_ref_raw, u_raw = {}, {}, {}, {}
        gain_packed, err, err_packed, u_turned, y_turned, y_packed, y_rows, y_codes = ({} for k in range(8))

        free_banks = list(range(BANKS))
        filled = {}

        def take_bank(key, shape):
            bank = free_banks[0]
            free_banks.remove(bank)
            tile = psum.tile(shape, F32, name="bank_%d" % bank)
            filled[key] = (bank, tile)
            return tile

        def empty_bank(key):
            bank, tile = filled[key]
            free_banks.append(bank)
            return tile

        def copy(engine, dst, src):
            if engine == "V":
                nc.vector.tensor_copy(out=dst, in_=src)
            else:
                nc.scalar.copy(out=dst, in_=src)

        def load_limits():
            nc.sync.dma_start(out=limits_raw[:, 0, :, :], in_=u_lo.rearrange("(g p t) -> p g t", p=P, t=PACK))
            nc.sync.dma_start(out=limits_raw[:, 1, :, :], in_=u_hi.rearrange("(g p t) -> p g t", p=P, t=PACK))

        def widen_limits():
            nc.gpsimd.tensor_copy(out=limits[:], in_=limits_raw[:])

        def load_gain(kp, g0, count):
            tile = keep.tile([P, PACK, count * GROUP], BF16, name="gain_raw_%d_%d" % (kp, g0))
            src = gain[kp * GROUP:(kp + 1) * GROUP, g0 * GROUP:(g0 + count) * GROUP]
            nc.sync.dma_start(out=tile[:], in_=src.rearrange("(p j) n -> p j n", j=PACK))
            for g in range(count):
                gain_raw[kp, g0 + g] = tile[:, :, g * GROUP:(g + 1) * GROUP]

        def load_states(c):
            for src, tiles, name in ((x, x_raw, "x_raw"), (x_ref, x_ref_raw, "x_ref_raw")):
                tiles[c] = work.tile([P, B, S], BF16, name=name, bufs=2)
                rows = src[c * ROWS:(c + 1) * ROWS, :]
                nc.sync.dma_start(out=tiles[c][:], in_=rows.rearrange("(r b) k -> r b k", b=B))

        def load_u(c, g0, count):
            tile = keep.tile([P, B, count * GROUP], BF16, name="u_raw_%d_%d" % (c, g0))
            src = u_ref[c * ROWS:(c + 1) * ROWS, g0 * GROUP:(g0 + count) * GROUP]
            nc.sync.dma_start(out=tile[:], in_=src.rearrange("(r b) n -> r b n", b=B))
            for g in range(count):
                u_raw[c, g0 + g] = tile[:, :, g * GROUP:(g + 1) * GROUP]

        def pack_gain(engine, kp, g):
            gain_packed[kp, g] = work.tile([P, PACK, P, PACK], BF16, name="gain_packed", align_bytes=64, bufs=2)
            copy(engine, gain_packed[kp, g][:].rearrange("p t m j -> p m j t"),
                 gain_raw[kp, g].rearrange("p j (m t) -> p m j t", t=PACK))

        def quantize_gain(kp, g):
            cols = slice(g * GROUP, (g + 1) * GROUP)
            nc.vector.quantize_mx(out=gain_codes[:, kp, cols].bitcast(FP8X4), scales=gain_scales[:, kp, cols],
                                  in_=gain_packed[kp, g][:].rearrange("p t m j -> p (t m j)"))

        def subtract(c):
            err[c] = work.tile([P, 2, B * S // 2], BF16, name="err", bufs=2)
            pairs = "r b (q u e) -> r u (b q) e"
            nc.vector.tensor_tensor(out=err[c][:].rearrange("r u (q e) -> r u q e", e=2),
                                    in0=x_ref_raw[c][:].rearrange(pairs, u=2, e=2),
                                    in1=x_raw[c][:].rearrange(pairs, u=2, e=2), op=ALU.subtract)

        def turn_err(c, kp):
            bank = take_bank(("err", c, kp), [P, 2, B, P])
            words = err[c][:].bitcast(F32)
            for u in range(2):
                for b in range(B):
                    q0 = (b * KP + kp) * P
                    nc.tensor.transpose(bank[:, u, b, :], words[:, u, q0:q0 + P], ident[:])

        def copy_err(engine, c, kp):
            c0, w = ERR_SPAN[c]
            if c == c0:
                err_packed[c0, kp] = work.tile([P, w * ROWS * PACK], BF16, name="err_packed", align_bytes=64,
                                               bufs=2)
            dst = err_packed[c0, kp][:, (c - c0) * ROWS * PACK:(c - c0 + 1) * ROWS * PACK]
            copy(engine, dst.bitcast(F32).rearrange("p (r b u) -> p r b u", b=B, u=2),
                 empty_bank(("err", c, kp))[:].rearrange("p u b r -> p r b u"))

        def quantize_err(c, kp):
            cols = slice(c * ROWS, (c + ERR_SPAN[c][1]) * ROWS)
            nc.vector.quantize_mx(out=err_codes[:, kp, cols].bitcast(FP8X4), scales=err_scales[:, kp, cols],
                                  in_=err_packed[c, kp][:])

        def turn_u(c, g):
            bank = take_bank(("u", c, g), [P, 2, B, P])
            for b in range(B):
                words = u_raw[c, g][:, b, :].bitcast(F32)
                for u in range(2):
                    nc.tensor.transpose(bank[:, u, b, :], words[:, u::2], ident[:])

        def copy_u(engine, c, g):
            c0, w = unit_of[c, g]
            if c == c0:
                u_turned[c0, g] = work.tile([P, 2, w * ROWS * 2], BF16, name="u_turned", bufs=3)
            dst = u_turned[c0, g][:, :, (c - c0) * ROWS * 2:(c - c0 + 1) * ROWS * 2]
            copy(engine, dst.bitcast(F32).rearrange("p u (r b) -> p u r b", b=B),
                 empty_bank(("u", c, g))[:].rearrange("p u b r -> p u r b"))

        def multiply(c, g, i):
            w = unit_of[c, g][1]
            slots = 2 // w
            rows = slice(c * ROWS, (c + w) * ROWS)
            bank = take_bank(("fb", c, g, i), [P, slots, w * ROWS])
            for e in range(slots):
                n0 = g * GROUP + (slots * i + e) * P
                for kp in range(KP):
                    nc.tensor.matmul_mx(
                        out=bank[:, e, :],
                        lhsT=gain_codes[:, kp, n0:n0 + P].bitcast(FP8X4),
                        lhsT_scale=gain_scales[:, kp, n0:n0 + P],
                        rhs=err_codes[:, kp, rows].bitcast(FP8X4),
                        rhs_scale=err_scales[:, kp, rows],
                        start=(kp == 0), stop=(kp == KP - 1))

        def add_u(c, g, i):
            w = unit_of[c, g][1]
            slots = 2 // w
            if i == 0:
                y_turned[c, g] = work.tile([P, PACK, w * ROWS], F32, name="y_turned", bufs=3)
            t0 = slots * i
            u_pair = u_turned[c, g][:, t0 // 2, :].rearrange("p (m e) -> p e m", e=2)
            nc.vector.tensor_tensor(out=y_turned[c, g][:, t0:t0 + slots, :], in0=empty_bank(("fb", c, g, i))[:],
                                    in1=u_pair[:, t0 % 2:t0 % 2 + slots, :], op=ALU.add)

        def limit(engine, c, g, t):
            values = y_turned[c, g][:, t, :]
            builder = nc.vector if engine == "V" else nc.gpsimd
            builder.tensor_scalar(out=values, in0=values, scalar1=limits[:, 1, g, t:t + 1],
                                  scalar2=limits[:, 0, g, t:t + 1], op0=ALU.min, op1=ALU.max)

        def pack_y(engine, c, g):
            c0, w = unit_of[c, g]
            if c == c0:
                y_packed[c0, g] = work.tile([P, w * ROWS * PACK], BF16, name="y_packed", align_bytes=64, bufs=3)
            m0 = (c - c0) * ROWS
            dst = y_packed[c0, g][:, m0 * PACK:(m0 + ROWS) * PACK].rearrange("p (m i t) -> p m t i", i=2, t=PACK)
            copy(engine, dst, y_turned[c0, g][:, :, m0:m0 + ROWS].rearrange("p t (m i) -> p m t i", i=2))

        def quantize_y(c, g):
            w = unit_of[c, g][1]
            if g % 2 == 0:
                y_codes[c, g // 2] = work.tile([P, 2, w * ROWS], U32, name="y_codes", align_bytes=64, bufs=3)
            i = scale_set_of[c, g]
            m0 = (c - SCALE_SETS[i][0]) * ROWS
            nc.vector.quantize_mx(out=y_codes[c, g // 2][:, g % 2, :].bitcast(FP8X4),
                                  scales=y_scales[i][:, g - SCALE_SETS[i][2], m0:m0 + w * ROWS], in_=y_packed[c, g][:])

        def turn_y(c, g, b):
            bank = take_bank(("y", c, g, b), [P, PACK, P])
            c0 = unit_of[c, g][0]
            m0 = (c - c0) * ROWS + b * P
            for t in range(PACK):
                nc.tensor.transpose(bank[:, t, :], y_turned[c0, g][:, t, m0:m0 + P], ident[:])

        def copy_y(engine, c, g, b):
            if g % 2 == 0 and b == 0:
                y_rows[c, g // 2] = work.tile([P, B, 2 * GROUP], F32, name="y_rows", bufs=4)
            dst = y_rows[c, g // 2][:, b, (g % 2) * GROUP:(g % 2 + 1) * GROUP]
            copy(engine, dst.rearrange("m (p t) -> m p t", t=PACK),
                 empty_bank(("y", c, g, b))[:].rearrange("m t p -> m p t"))

        def store_y(c, g, count, b0, b1):
            src = y_rows[c, g // 2][:, b0:b1, (g % 2 + 1 - count) * GROUP:(g % 2 + 1) * GROUP]
            dst = out_0[c * ROWS + b0 * P:c * ROWS + b1 * P, (g + 1 - count) * GROUP:(g + 1) * GROUP]
            nc.sync.dma_start(out=dst.rearrange("(b m) n -> m b n", m=P), in_=src)

        def store_codes(c, g, count):
            rows = slice(c * ROWS, (c + unit_of[c, g][1]) * ROWS)
            dst = out_1[g + 1 - count:g + 1, :, rows, :].rearrange("g p m t -> p g (m t)")
            src = y_codes[c, g // 2][:, g % 2 + 1 - count:g % 2 + 1, :]
            nc.sync.dma_start(out=dst.bitcast(I32), in_=src.bitcast(I32))

        def store_scales(i):
            c0, c1, g0, g1 = SCALE_SETS[i]
            queue = nc.scalar if i == len(SCALE_SETS) - 1 else nc.sync
            for q in range(P // 32):
                dst = out_2[g0:g1, 4 * q:4 * q + 4, c0 * ROWS:c1 * ROWS].rearrange("g r m -> r g m")
                queue.dma_start(out=dst.bitcast(I32), in_=y_scales[i][32 * q:32 * q + 4, :, :].bitcast(I32))

        make_identity(nc, ident[:])

        steps = {"ll": load_limits, "wl": widen_limits, "lg": load_gain, "lx": load_states, "lu": load_u,
                 "pg": pack_gain, "qg": quantize_gain,
                 "sub": subtract, "te": turn_err, "ce": copy_err, "qe": quantize_err,
                 "tu": turn_u, "cu": copy_u, "mm": multiply, "add": add_u, "lim": limit,
                 "py": pack_y, "qy": quantize_y, "ty": turn_y, "cy": copy_y,
                 "sy": store_y, "sc": store_codes, "ss": store_scales}
        for step in ORDER.split():
            name, args = step.split(":")
            steps[name](*[a if a in "VSG" else int(a) for a in args])
